import numpy as np, ml_dtypes
CORES = [24,40,56,80,88,96]
N = 6
import mx_ref
NC, G = 256, 2
C = np.float32(0.00048828125)
BF = ml_dtypes.bfloat16
def cut(t, i, w=512):
    return t[:, w * i:w * i + w]
def tile(rs):
    return np.stack(rs, axis=2).reshape(128, -1).astype(BF)
def layer(w, X):
    out = []
    for i in range(G):
        for t in range(len(X)):
            p = mx_ref.matmul(mx_ref.quantize(cut(w, len(X) * i + t)), X[t])
            z = p if t == 0 else z + p
        out.append(z)
    return out
def gate(U, V):
    return [(np.maximum(s * u, 0) * v) * C for u, v in zip(U, V) for s in (1, -1)]
def setup_inputs(rng):
    def f(*shape):
        return mx_ref.flush((rng.standard_normal(shape, dtype=np.float32) * np.exp2(rng.integers(-2, 3, shape[:-1] + (1,)))).astype(BF))
    return {"x": f(N, 128, 4 * NC), "u": f(N, 128, G * 512), "v": f(N, 128, G * 512), "w2": f(N, 128, N * 512)}
def setup_inputs_blocks(rng):
    d = setup_inputs(rng)
    for k in ("x", "u", "v", "w2"): d[k] = mx_ref.spread(d[k], rng, 2)
    return d
def setup_inputs_wide(rng):
    d = setup_inputs(rng)
    for k in ("x", "u", "v", "w2"): d[k] = mx_ref.flush((d[k].astype(np.float32) * np.exp2(rng.integers(-5, 6, (N, 1, 1))).astype(np.float32)).astype(BF))
    return d
def setup_inputs_zeros(rng):
    d = setup_inputs(rng); v = d["x"].reshape(N, 128, -1, 4).copy()
    v[np.broadcast_to((rng.random((N, 1, v.shape[2], 1)) < 0.33), v.shape)] = 0
    d["x"] = v.reshape(d["x"].shape)
    return d
def reference(x, u, v, w2):
    h = np.zeros((N, 128, 4 * NC), BF)
    for j in range(N):
        X = [mx_ref.quantize(x[j])]
        h[j] = tile(gate(layer(u[j], X), layer(v[j], X)))
    H = [mx_ref.quantize(h[j]) for j in range(N)]
    y = np.zeros((N, 128, NC), np.float32)
    for r in range(N):
        for j in range(N):
            p = mx_ref.matmul(mx_ref.quantize(cut(w2[r], j)), H[j])
            y[r] = p if j == 0 else y[r] + p
    return {"y": y}

@@ -1,0 +1,256 @@
+from concourse.bass import DstId, RemoteDMATransfer
+from concourse.mybir import dt, AluOpType, ActivationFunctionType
+
+N = 6
+NC = 256
+HC = NC // 2
+C = 0.00048828125
+
+SCRATCH = {
+    "xb": ("sbuf", [128, 4 * NC], "bfloat16"),
+    "ub": ("sbuf", [128, 1024], "bfloat16"),
+    "vb": ("sbuf", [128, 1024], "bfloat16"),
+    "wb": ("sbuf", [128, N * 512], "bfloat16"),
+    "xq": ("sbuf", [128, NC], "float8_e4m3fn_x4"),
+    "xs": ("sbuf", [128, NC], "uint8"),
+    "uq": ("sbuf", [128, 256], "float8_e4m3fn_x4"),
+    "us": ("sbuf", [128, 256], "uint8"),
+    "vq": ("sbuf", [128, 256], "float8_e4m3fn_x4"),
+    "vs": ("sbuf", [128, 256], "uint8"),
+    "wq": ("sbuf", [128, N * 128], "float8_e4m3fn_x4"),
+    "ws": ("sbuf", [128, N * 128], "uint8"),
+    "a": ("sbuf", [128, 4 * NC], "float32"),
+    "hb": ("sbuf", [128, 4 * NC], "bfloat16"),
+    "hq": ("sbuf", [128, N * NC], "float8_e4m3fn_x4"),
+    "hs": ("sbuf", [128, N * NC], "uint8"),
+    "ps": ("psum", [128, 512 * 6], "float32"),
+    "yb": ("sbuf", [128, NC], "float32"),
+}
+SEMAPHORES = (["lx", "lu", "lv", "lw", "qx", "qu0", "qu1", "qv0", "qv1", "mu0", "mu1", "mv0", "mv1",
+               "r0", "r1", "r2", "r3", "hm", "qh", "qw", "y0", "y1", "yc", "st", "sent"]
+              + ["s%d" % j for j in range(N)] + ["c%d" % j for j in range(N)])
+
+_PLAN = {}
+
+
+def _bits(mask):
+    return bin(mask).count("1")
+
+
+def _links(topo, k, d):
+    a, b, e = topo.chip(k), topo.chip(d), topo.die(k)
+    if a == b:
+        return []
+    if topo.same_plane(a, b):
+        return [("out", a, e), ("in", b, e)]
+    if topo.mates(a, b):
+        return [("mate", a, b, e)]
+    m = [c for c in range(topo.CHIPS) if topo.mates(a, c)][0]
+    return [("mate", a, m, e), ("out", m, e), ("in", b, e)]
+
+
+def _choices(topo, cores, s):
+    cs, n = cores[s], len(cores)
+    others = [(s + i) % n for i in range(1, n)]
+    near = [d for d in others if topo.may_write(cs, cores[d])]
+    far = [d for d in others if d not in near]
+    here = [k for k in range(topo.CHIPS * topo.CORES_PER_CHIP) if topo.chip(k) == topo.chip(cs) and k != cs]
+    dies = sorted({topo.die(k) for k in here})
+    out = []
+    for i in range(len(far)):
+        for j in range(len(far)):
+            if i == j:
+                continue
+            pair = [far[i], far[j]]
+            rest = [d for d in far if d not in pair]
+            for singles in ([rest] if rest else [[d] for d in near]):
+                jobs = [pair] + [[d] for d in singles]
+                left = [d for d in near if d not in singles]
+                for direct in ([left, left[::-1]] if len(left) > 1 else [left]):
+                    for code in range(len(dies) ** len(jobs)):
+                        used = []
+                        for q, job in enumerate(jobs):
+                            e = dies[(code // len(dies) ** q) % len(dies)]
+                            fit = [k for k in here if topo.die(k) == e and k not in used
+                                   and all(topo.may_write(k, cores[d]) for d in job)]
+                            if not fit:
+                                break
+                            used.append(fit[0])
+                        if len(used) == len(jobs):
+                            out.append((direct, list(zip(used, jobs))))
+    return out
+
+
+def _score(topo, cores, share):
+    load, meet = {}, {}
+    for s, (direct, jobs) in enumerate(share):
+        flows = [(cores[s], d, len(jobs) - 2 + i) for i, d in enumerate(direct)]
+        flows += [(jobs[0][0], d, 1 + i) for i, d in enumerate(jobs[0][1])]
+        flows += [(k, ds[0], 2) for k, ds in jobs[1:]]
+        for k, d, phase in flows:
+            for p in _links(topo, k, cores[d]):
+                load[p] = load.get(p, 0) + 1
+                meet[(p, phase)] = meet.get((p, phase), 0) + 1
+    return sorted(load.values(), reverse=True), sorted(meet.values(), reverse=True)
+
+
+def _plan(topo, cores):
+    if "p" in _PLAN:
+        return _PLAN["p"]
+    n = len(cores)
+    opts = [_choices(topo, cores, s) for s in range(n)]
+    share = [o[0] for o in opts]
+    for _ in range(6):
+        before = list(share)
+        for s in range(n):
+            share[s] = min(opts[s], key=lambda o: _score(topo, cores, share[:s] + [o] + share[s + 1:]))
+        if share == before:
+            break
+    waves, jobs, count, when = [], {}, {}, {}
+    hop = 0.7
+    for s in range(n):
+        cs = cores[s]
+        direct, helpers = share[s]
+        first, low, high = helpers[0], helpers[1:-1], helpers[-1]
+        low_t = [k for k, _ in low] + [cores[d] for d in direct]
+        m_first = topo.mask(cs, first[0])
+        m_low = m_first
+        for k in low_t:
+            m_low &= topo.mask(cs, k)
+        m_high = topo.mask(cs, high[0]) & ~m_low
+        if low:
+            waves.append([[(m_first, [first[0]])], [(m_low, [k for k, _ in low]), (m_high, [high[0]])],
+                          [(m_low, [cores[d] for d in direct])]])
+        else:
+            waves.append([[(m_first, [first[0]])], [(m_low, low_t), (m_high, [high[0]])]])
+        got = {first[0]: 0.5, high[0]: 1.5}
+        count[(first[0], s)], count[(high[0], s)] = _bits(m_first), _bits(m_high)
+        for i, k in enumerate(low_t):
+            got[k] = 1.5 + i
+            count[(k, s)] = _bits(m_low)
+        for d in direct:
+            when[(d, s)] = got[cores[d]]
+        for k, ds in helpers:
+            m = topo.mask(k, cores[ds[0]])
+            for d in ds:
+                m &= topo.mask(k, cores[d])
+            jobs[k] = (s, m, [cores[d] for d in ds])
+            for i, d in enumerate(ds):
+                count[(cores[d], s)] = _bits(m)
+                when[(d, s)] = got[k] + hop + 1 + i
+    order = [[r] + sorted([j for j in range(n) if j != r], key=lambda j: (when[(r, j)], j)) for r in range(n)]
+    _PLAN["p"] = {"waves": waves, "jobs": jobs, "count": count, "order": order}
+    return _PLAN["p"]
+
+
+def _send(g, T, topo, j, part, groups):
+    def view():
+        if part == "s":
+            return T.hs[:, NC * j:NC * j + NC]
+        return T.hq[:, NC * j:NC * j + NC].bitcast(dt.uint8)
+    there = T.sem["%s%d" % (part, j)]
+    if len(groups) == 1 and len(groups[0][1]) == 1:
+        mask, (d,) = groups[0]
+        rid, pid = topo.addr(d)[:2]
+        g.remote_dma(out_ap=view(), in_ap=view(), remote_sem=there, local_sem=T.sem.sent, pid=pid, routing_id=rid,
+                     dma_engine_mask=mask)
+        return _bits(mask)
+    trs = []
+    for mask, ds in groups:
+        ids = [DstId(rid=topo.addr(d)[0], pnc=topo.addr(d)[1]) for d in ds]
+        trs.append(RemoteDMATransfer(dst_ids=ids, dma_engine_mask=mask, remote_sem=there,
+                                     srcs=[view()], dsts=[view() for _ in ds]))
+    g.remote_dma_fused(trs, local_sem=T.sem.sent)
+    return sum(_bits(mask) for mask, _ in groups)
+
+
+def _helper(g, core, T, topo, plan):
+    j, mask, targets = plan["jobs"][core]
+    sent = 0
+    for part in ("s", "c"):
+        g.wait_ge(T.sem["%s%d" % (part, j)], plan["count"][(core, j)])
+        sent += _send(g, T, topo, j, part, [(mask, targets)])
+    g.wait_ge(T.sem.sent, sent)
+
+
+def rank_program(g, core, T, topo):
+    plan = _plan(topo, list(T.cores))
+    r = T.rank_of(core)
+    if r is None:
+        if core in plan["jobs"]:
+            _helper(g, core, T, topo, plan)
+        return
+    sem = T.sem
+    ve, te, se, sy = g.vector, g.tensor, g.scalar, g.sync
+
+    def bank(k, n):
+        return T.ps[:, 512 * k:512 * k + n]
+
+    sy.dma_start(T.xb[:], T.x[:]).then_inc(sem.lx, 16)
+    se.dma_start(T.ub[:], T.u[:]).then_inc(sem.lu, 16)
+    sy.dma_start(T.vb[:], T.v[:]).then_inc(sem.lv, 16)
+    sy.dma_start(T.wb[:], T.w2[:]).then_inc(sem.lw, 16)
+
+    ve.wait_ge(sem.lx, 16)
+    ve.quantize_mx(T.xq[:], T.xs[:], T.xb[:]).then_inc(sem.qx, 1)
+    for name, q, s, b, l in (("qu", T.uq, T.us, T.ub, sem.lu), ("qv", T.vq, T.vs, T.vb, sem.lv)):
+        ve.wait_ge(l, 16)
+        for i in range(2):
+            ve.quantize_mx(q[:, 128 * i:128 * i + 128], s[:, 128 * i:128 * i + 128],
+                           b[:, 512 * i:512 * i + 512]).then_inc(sem["%s%d" % (name, i)], 1)
+
+    te.wait_ge(sem.qx, 1)
+    for k, (name, q, s) in enumerate((("u", T.uq, T.us), ("v", T.vq, T.vs))):
+        for i in range(2):
+            te.wait_ge(sem["q%s%d" % (name, i)], 1)
+            te.matmul_mx(bank(2 * k + i, NC), q[:, 128 * i:128 * i + 128], s[:, 128 * i:128 * i + 128],
+                         T.xq[:], T.xs[:], True, True).then_inc(sem["m%s%d" % (name, i)], 1)
+
+    for b in range(4):
+        if b % 2 == 0:
+            se.wait_ge(sem["mu%d" % (b // 2)], 1)
+        se.activation(T.a[:, NC * b:NC * b + NC], bank(b // 2, NC), ActivationFunctionType.Relu,
+                      scale=(C if b % 2 == 0 else -C)).then_inc(sem["r%d" % b], 1)
+
+    for b in range(4):
+        ve.wait_ge(sem["r%d" % b], 1)
+        if b % 2 == 0:
+            ve.wait_ge(sem["mv%d" % (b // 2)], 1)
+        ve.tensor_tensor(T.hb[:, b:4 * NC:4], T.a[:, NC * b:NC * b + NC], bank(2 + b // 2, NC),
+                         AluOpType.mult).then_inc(sem.hm, 1)
+    ve.wait_ge(sem.hm, 4)
+    ve.quantize_mx(T.hq[:, NC * r:NC * r + NC], T.hs[:, NC * r:NC * r + NC], T.hb[:]).then_inc(sem.qh, 1)
+
+    g.wait_ge(sem.qh, 1)
+    sent = 0
+    for wave in plan["waves"][r]:
+        for part in ("s", "c"):
+            sent += _send(g, T, topo, r, part, wave)
+    g.wait_ge(sem.sent, sent)
+
+    ve.wait_ge(sem.lw, 16)
+    for k in range(2):
+        w = N * 128 // 2
+        ve.quantize_mx(T.wq[:, w * k:w * k + w], T.ws[:, w * k:w * k + w],
+                       T.wb[:, 4 * w * k:4 * w * k + 4 * w]).then_inc(sem.qw, 1)
+
+    te.wait_ge(sem.qw, 2)
+    te.wait_ge(sem.qh, 1)
+    for n, j in enumerate(plan["order"][r]):
+        if j != r:
+            te.wait_ge(sem["s%d" % j], plan["count"][(core, j)])
+            te.wait_ge(sem["c%d" % j], plan["count"][(core, j)])
+        for h in range(2):
+            lo = NC * j + HC * h
+            mm = te.matmul_mx(bank(4 + h, HC), T.wq[:, 128 * j:128 * j + 128], T.ws[:, 128 * j:128 * j + 128],
+                              T.hq[:, lo:lo + HC], T.hs[:, lo:lo + HC], n == 0, n == N - 1)
+            if n == N - 1:
+                mm.then_inc(sem["y%d" % h], 1)
+
+    ve.wait_ge(sem.y0, 1)
+    ve.tensor_copy(T.yb[:, 0:HC], bank(4, HC)).then_inc(sem.yc, 1)
+    se.wait_ge(sem.y1, 1)
+    se.activation(T.yb[:, HC:NC], bank(5, HC), ActivationFunctionType.Copy).then_inc(sem.yc, 1)
+    sy.wait_ge(sem.yc, 2)
+    sy.dma_start(T.y[:], T.yb[:]).then_inc(sem.st, 16)
+    sy.wait_ge(sem.st, 16)

@@ -23,11 +23,13 @@ SCRATCH = {
     "hb": ("sbuf", [128, 4 * NC], "bfloat16"),
     "hq": ("sbuf", [128, N * NC], "float8_e4m3fn_x4"),
     "hs": ("sbuf", [128, N * NC], "uint8"),
-    "ps": ("psum", [128, 512 * 6], "float32"),
+    "ps": ("psum", [128, 512 * 8], "float32"),
     "yb": ("sbuf", [128, NC], "float32"),
 }
-SEMAPHORES = (["lx", "lu", "lv", "lw", "qx", "qu0", "qu1", "qv0", "qv1", "mu0", "mu1", "mv0", "mv1",
-               "r0", "r1", "r2", "r3", "hm", "qh", "qw", "y0", "y1", "yc", "st", "sent"]
+SEMAPHORES = (["lx", "lu", "lv", "lw", "qx0", "qx1", "qu0", "qu1", "qv0", "qv1", "hm0", "hm1", "qh0", "qh1",
+               "qw", "y0", "y1", "yc", "st", "sent"]
+              + ["m%s%d%d" % (k, i, h) for k in "uv" for i in range(2) for h in range(2)]
+              + ["r%d%d" % (b, h) for b in range(4) for h in range(2)]
               + ["s%d" % j for j in range(N)] + ["c%d" % j for j in range(N)])
 
 _PLAN = {}
@@ -138,16 +140,20 @@ def _plan(topo, cores):
             for i, d in enumerate(ds):
                 count[(cores[d], s)] = _bits(m)
                 when[(d, s)] = got[k] + hop + 1 + i
+    plane = dict(count)
+    for s in range(n):
+        k = waves[s][0][0][1][0]
+        plane[(k, s)] = 2 * count[(k, s)]
     order = [[r] + sorted([j for j in range(n) if j != r], key=lambda j: (when[(r, j)], j)) for r in range(n)]
-    _PLAN["p"] = {"waves": waves, "jobs": jobs, "count": count, "order": order}
+    _PLAN["p"] = {"waves": waves, "jobs": jobs, "count": count, "plane": plane, "order": order}
     return _PLAN["p"]
 
 
-def _send(g, T, topo, j, part, groups):
+def _send(g, T, topo, j, part, groups, lo=0, hi=NC):
     def view():
         if part == "s":
-            return T.hs[:, NC * j:NC * j + NC]
-        return T.hq[:, NC * j:NC * j + NC].bitcast(dt.uint8)
+            return T.hs[:, NC * j + lo:NC * j + hi]
+        return T.hq[:, NC * j + lo:NC * j + hi].bitcast(dt.uint8)
     there = T.sem["%s%d" % (part, j)]
     if len(groups) == 1 and len(groups[0][1]) == 1:
         mask, (d,) = groups[0]
@@ -167,8 +173,8 @@ def _send(g, T, topo, j, part, groups):
 def _helper(g, core, T, topo, plan):
     j, mask, targets = plan["jobs"][core]
     sent = 0
-    for part in ("s", "c"):
-        g.wait_ge(T.sem["%s%d" % (part, j)], plan["count"][(core, j)])
+    for part, need in (("s", plan["plane"]), ("c", plan["count"])):
+        g.wait_ge(T.sem["%s%d" % (part, j)], need[(core, j)])
         sent += _send(g, T, topo, j, part, [(mask, targets)])
     g.wait_ge(T.sem.sent, sent)
 
@@ -183,8 +189,12 @@ def rank_program(g, core, T, topo):
     sem = T.sem
     ve, te, se, sy = g.vector, g.tensor, g.scalar, g.sync
 
-    def bank(k, n):
-        return T.ps[:, 512 * k:512 * k + n]
+    def bank(k):
+        return T.ps[:, 512 * k:512 * k + HC]
+
+    def quant(q, s, b, k, done):
+        ve.quantize_mx(q[:, 128 * k:128 * k + 128], s[:, 128 * k:128 * k + 128],
+                       b[:, 512 * k:512 * k + 512]).then_inc(done, 1)
 
     sy.dma_start(T.xb[:], T.x[:]).then_inc(sem.lx, 16)
     se.dma_start(T.ub[:], T.u[:]).then_inc(sem.lu, 16)
@@ -192,38 +202,52 @@ def rank_program(g, core, T, topo):
     sy.dma_start(T.wb[:], T.w2[:]).then_inc(sem.lw, 16)
 
     ve.wait_ge(sem.lx, 16)
-    ve.quantize_mx(T.xq[:], T.xs[:], T.xb[:]).then_inc(sem.qx, 1)
-    for name, q, s, b, l in (("qu", T.uq, T.us, T.ub, sem.lu), ("qv", T.vq, T.vs, T.vb, sem.lv)):
-        ve.wait_ge(l, 16)
-        for i in range(2):
-            ve.quantize_mx(q[:, 128 * i:128 * i + 128], s[:, 128 * i:128 * i + 128],
-                           b[:, 512 * i:512 * i + 512]).then_inc(sem["%s%d" % (name, i)], 1)
+    quant(T.xq, T.xs, T.xb, 0, sem.qx0)
+    ve.wait_ge(sem.lu, 16)
+    quant(T.uq, T.us, T.ub, 0, sem.qu0)
+    quant(T.uq, T.us, T.ub, 1, sem.qu1)
+    quant(T.xq, T.xs, T.xb, 1, sem.qx1)
+    ve.wait_ge(sem.lv, 16)
+    quant(T.vq, T.vs, T.vb, 0, sem.qv0)
+    quant(T.vq, T.vs, T.vb, 1, sem.qv1)
 
-    te.wait_ge(sem.qx, 1)
     for k, (name, q, s) in enumerate((("u", T.uq, T.us), ("v", T.vq, T.vs))):
-        for i in range(2):
-            te.wait_ge(sem["q%s%d" % (name, i)], 1)
-            te.matmul_mx(bank(2 * k + i, NC), q[:, 128 * i:128 * i + 128], s[:, 128 * i:128 * i + 128],
-                         T.xq[:], T.xs[:], True, True).then_inc(sem["m%s%d" % (name, i)], 1)
+        for h in range(2):
+            te.wait_ge(sem["qx%d" % h], 1)
+            for i in range(2):
+                te.wait_ge(sem["q%s%d" % (name, i)], 1)
+                te.matmul_mx(bank(4 * k + 2 * h + i), q[:, 128 * i:128 * i + 128], s[:, 128 * i:128 * i + 128],
+                             T.xq[:, HC * h:HC * h + HC], T.xs[:, HC * h:HC * h + HC],
+                             True, True).then_inc(sem["m%s%d%d" % (name, i, h)], 1)
 
-    for b in range(4):
-        if b % 2 == 0:
-            se.wait_ge(sem["mu%d" % (b // 2)], 1)
-        se.activation(T.a[:, NC * b:NC * b + NC], bank(b // 2, NC), ActivationFunctionType.Relu,
-                      scale=(C if b % 2 == 0 else -C)).then_inc(sem["r%d" % b], 1)
+    for h in range(2):
+        for b in range(4):
+            if b % 2 == 0:
+                se.wait_ge(sem["mu%d%d" % (b // 2, h)], 1)
+            lo = NC * b + HC * h
+            se.activation(T.a[:, lo:lo + HC], bank(2 * h + b // 2), ActivationFunctionType.Relu,
+                          scale=(C if b % 2 == 0 else -C)).then_inc(sem["r%d%d" % (b, h)], 1)
 
-    for b in range(4):
-        ve.wait_ge(sem["r%d" % b], 1)
-        if b % 2 == 0:
-            ve.wait_ge(sem["mv%d" % (b // 2)], 1)
-        ve.tensor_tensor(T.hb[:, b:4 * NC:4], T.a[:, NC * b:NC * b + NC], bank(2 + b // 2, NC),
-                         AluOpType.mult).then_inc(sem.hm, 1)
-    ve.wait_ge(sem.hm, 4)
-    ve.quantize_mx(T.hq[:, NC * r:NC * r + NC], T.hs[:, NC * r:NC * r + NC], T.hb[:]).then_inc(sem.qh, 1)
+    for h in range(2):
+        for b in range(4):
+            ve.wait_ge(sem["r%d%d" % (b, h)], 1)
+            if b % 2 == 0:
+                ve.wait_ge(sem["mv%d%d" % (b // 2, h)], 1)
+            lo = NC * b + HC * h
+            ve.tensor_tensor(T.hb[:, 4 * HC * h + b:4 * HC * h + 4 * HC:4], T.a[:, lo:lo + HC],
+                             bank(4 + 2 * h + b // 2), AluOpType.mult).then_inc(sem["hm%d" % h], 1)
+        ve.wait_ge(sem["hm%d" % h], 4)
+        lo = NC * r + HC * h
+        ve.quantize_mx(T.hq[:, lo:lo + HC], T.hs[:, lo:lo + HC],
+                       T.hb[:, 4 * HC * h:4 * HC * h + 4 * HC]).then_inc(sem["qh%d" % h], 1)
 
-    g.wait_ge(sem.qh, 1)
-    sent = 0
-    for wave in plan["waves"][r]:
+    first = plan["waves"][r][0]
+    g.wait_ge(sem.qh0, 1)
+    sent = _send(g, T, topo, r, "s", first, 0, HC)
+    g.wait_ge(sem.qh1, 1)
+    sent += _send(g, T, topo, r, "s", first, HC, NC)
+    sent += _send(g, T, topo, r, "c", first)
+    for wave in plan["waves"][r][1:]:
         for part in ("s", "c"):
             sent += _send(g, T, topo, r, part, wave)
     g.wait_ge(sem.sent, sent)
@@ -235,22 +259,25 @@ def rank_program(g, core, T, topo):
                        T.wb[:, 4 * w * k:4 * w * k + 4 * w]).then_inc(sem.qw, 1)
 
     te.wait_ge(sem.qw, 2)
-    te.wait_ge(sem.qh, 1)
+    te.wait_ge(sem.qh0, 1)
+    te.wait_ge(sem.qh1, 1)
+    for b in range(4):
+        te.wait_ge(sem["r%d0" % b], 1)
     for n, j in enumerate(plan["order"][r]):
         if j != r:
-            te.wait_ge(sem["s%d" % j], plan["count"][(core, j)])
+            te.wait_ge(sem["s%d" % j], plan["plane"][(core, j)])
             te.wait_ge(sem["c%d" % j], plan["count"][(core, j)])
         for h in range(2):
             lo = NC * j + HC * h
-            mm = te.matmul_mx(bank(4 + h, HC), T.wq[:, 128 * j:128 * j + 128], T.ws[:, 128 * j:128 * j + 128],
+            mm = te.matmul_mx(bank(h), T.wq[:, 128 * j:128 * j + 128], T.ws[:, 128 * j:128 * j + 128],
                               T.hq[:, lo:lo + HC], T.hs[:, lo:lo + HC], n == 0, n == N - 1)
             if n == N - 1:
                 mm.then_inc(sem["y%d" % h], 1)
 
     ve.wait_ge(sem.y0, 1)
-    ve.tensor_copy(T.yb[:, 0:HC], bank(4, HC)).then_inc(sem.yc, 1)
+    ve.tensor_copy(T.yb[:, 0:HC], bank(0)).then_inc(sem.yc, 1)
     se.wait_ge(sem.y1, 1)
-    se.activation(T.yb[:, HC:NC], bank(5, HC), ActivationFunctionType.Copy).then_inc(sem.yc, 1)
+    se.activation(T.yb[:, HC:NC], bank(1), ActivationFunctionType.Copy).then_inc(sem.yc, 1)
     sy.wait_ge(sem.yc, 2)
     sy.dma_start(T.y[:], T.yb[:]).then_inc(sem.st, 16)
     sy.wait_ge(sem.st, 16)

from concourse.bass import DstId, RemoteDMATransfer
from concourse.mybir import dt, AluOpType, ActivationFunctionType

N = 6
NC = 256
HC = NC // 2
C = 0.00048828125

SCRATCH = {
    "xb": ("sbuf", [128, 4 * NC], "bfloat16"),
    "ub": ("sbuf", [128, 1024], "bfloat16"),
    "vb": ("sbuf", [128, 1024], "bfloat16"),
    "wb": ("sbuf", [128, N * 512], "bfloat16"),
    "xq": ("sbuf", [128, NC], "float8_e4m3fn_x4"),
    "xs": ("sbuf", [128, NC], "uint8"),
    "uq": ("sbuf", [128, 256], "float8_e4m3fn_x4"),
    "us": ("sbuf", [128, 256], "uint8"),
    "vq": ("sbuf", [128, 256], "float8_e4m3fn_x4"),
    "vs": ("sbuf", [128, 256], "uint8"),
    "wq": ("sbuf", [128, N * 128], "float8_e4m3fn_x4"),
    "ws": ("sbuf", [128, N * 128], "uint8"),
    "a": ("sbuf", [128, 4 * NC], "float32"),
    "hb": ("sbuf", [128, 4 * NC], "bfloat16"),
    "hq": ("sbuf", [128, N * NC], "float8_e4m3fn_x4"),
    "hs": ("sbuf", [128, N * NC], "uint8"),
    "ps": ("psum", [128, 512 * 8], "float32"),
    "yb": ("sbuf", [128, NC], "float32"),
}
SEMAPHORES = (["lx", "lu", "lv", "lw", "qx0", "qx1", "qu0", "qu1", "qv0", "qv1", "hm0", "hm1", "qh0", "qh1",
               "qw", "y0", "y1", "yc", "st", "sent"]
              + ["m%s%d%d" % (k, i, h) for k in "uv" for i in range(2) for h in range(2)]
              + ["r%d%d" % (b, h) for b in range(4) for h in range(2)]
              + ["s%d" % j for j in range(N)] + ["c%d" % j for j in range(N)])

_PLAN = {}


def _bits(mask):
    return bin(mask).count("1")


def _links(topo, k, d):
    a, b, e = topo.chip(k), topo.chip(d), topo.die(k)
    if a == b:
        return []
    if topo.same_plane(a, b):
        return [("out", a, e), ("in", b, e)]
    if topo.mates(a, b):
        return [("mate", a, b, e)]
    m = [c for c in range(topo.CHIPS) if topo.mates(a, c)][0]
    return [("mate", a, m, e), ("out", m, e), ("in", b, e)]


def _choices(topo, cores, s):
    cs, n = cores[s], len(cores)
    others = [(s + i) % n for i in range(1, n)]
    near = [d for d in others if topo.may_write(cs, cores[d])]
    far = [d for d in others if d not in near]
    here = [k for k in range(topo.CHIPS * topo.CORES_PER_CHIP) if topo.chip(k) == topo.chip(cs) and k != cs]
    dies = sorted({topo.die(k) for k in here})
    out = []
    for i in range(len(far)):
        for j in range(len(far)):
            if i == j:
                continue
            pair = [far[i], far[j]]
            rest = [d for d in far if d not in pair]
            for singles in ([rest] if rest else [[d] for d in near]):
                jobs = [pair] + [[d] for d in singles]
                left = [d for d in near if d not in singles]
                for direct in ([left, left[::-1]] if len(left) > 1 else [left]):
                    for code in range(len(dies) ** len(jobs)):
                        used = []
                        for q, job in enumerate(jobs):
                            e = dies[(code // len(dies) ** q) % len(dies)]
                            fit = [k for k in here if topo.die(k) == e and k not in used
                                   and all(topo.may_write(k, cores[d]) for d in job)]
                            if not fit:
                                break
                            used.append(fit[0])
                        if len(used) == len(jobs):
                            out.append((direct, list(zip(used, jobs))))
    return out


def _score(topo, cores, share):
    load, meet = {}, {}
    for s, (direct, jobs) in enumerate(share):
        flows = [(cores[s], d, len(jobs) - 2 + i) for i, d in enumerate(direct)]
        flows += [(jobs[0][0], d, 1 + i) for i, d in enumerate(jobs[0][1])]
        flows += [(k, ds[0], 2) for k, ds in jobs[1:]]
        for k, d, phase in flows:
            for p in _links(topo, k, cores[d]):
                load[p] = load.get(p, 0) + 1
                meet[(p, phase)] = meet.get((p, phase), 0) + 1
    return sorted(load.values(), reverse=True), sorted(meet.values(), reverse=True)


def _plan(topo, cores):
    if "p" in _PLAN:
        return _PLAN["p"]
    n = len(cores)
    opts = [_choices(topo, cores, s) for s in range(n)]
    share = [o[0] for o in opts]
    for _ in range(6):
        before = list(share)
        for s in range(n):
            share[s] = min(opts[s], key=lambda o: _score(topo, cores, share[:s] + [o] + share[s + 1:]))
        if share == before:
            break
    waves, jobs, count, when = [], {}, {}, {}
    hop = 0.7
    for s in range(n):
        cs = cores[s]
        direct, helpers = share[s]
        first, low, high = helpers[0], helpers[1:-1], helpers[-1]
        low_t = [k for k, _ in low] + [cores[d] for d in direct]
        m_first = topo.mask(cs, first[0])
        m_low = m_first
        for k in low_t:
            m_low &= topo.mask(cs, k)
        m_high = topo.mask(cs, high[0]) & ~m_low
        if low:
            waves.append([[(m_first, [first[0]])], [(m_low, [k for k, _ in low]), (m_high, [high[0]])],
                          [(m_low, [cores[d] for d in direct])]])
        else:
            waves.append([[(m_first, [first[0]])], [(m_low, low_t), (m_high, [high[0]])]])
        got = {first[0]: 0.5, high[0]: 1.5}
        count[(first[0], s)], count[(high[0], s)] = _bits(m_first), _bits(m_high)
        for i, k in enumerate(low_t):
            got[k] = 1.5 + i
            count[(k, s)] = _bits(m_low)
        for d in direct:
            when[(d, s)] = got[cores[d]]
        for k, ds in helpers:
            m = topo.mask(k, cores[ds[0]])
            for d in ds:
                m &= topo.mask(k, cores[d])
            jobs[k] = (s, m, [cores[d] for d in ds])
            for i, d in enumerate(ds):
                count[(cores[d], s)] = _bits(m)
                when[(d, s)] = got[k] + hop + 1 + i
    plane = dict(count)
    for s in range(n):
        k = waves[s][0][0][1][0]
        plane[(k, s)] = 2 * count[(k, s)]
    order = [[r] + sorted([j for j in range(n) if j != r], key=lambda j: (when[(r, j)], j)) for r in range(n)]
    _PLAN["p"] = {"waves": waves, "jobs": jobs, "count": count, "plane": plane, "order": order}
    return _PLAN["p"]


def _send(g, T, topo, j, part, groups, lo=0, hi=NC):
    def view():
        if part == "s":
            return T.hs[:, NC * j + lo:NC * j + hi]
        return T.hq[:, NC * j + lo:NC * j + hi].bitcast(dt.uint8)
    there = T.sem["%s%d" % (part, j)]
    if len(groups) == 1 and len(groups[0][1]) == 1:
        mask, (d,) = groups[0]
        rid, pid = topo.addr(d)[:2]
        g.remote_dma(out_ap=view(), in_ap=view(), remote_sem=there, local_sem=T.sem.sent, pid=pid, routing_id=rid,
                     dma_engine_mask=mask)
        return _bits(mask)
    trs = []
    for mask, ds in groups:
        ids = [DstId(rid=topo.addr(d)[0], pnc=topo.addr(d)[1]) for d in ds]
        trs.append(RemoteDMATransfer(dst_ids=ids, dma_engine_mask=mask, remote_sem=there,
                                     srcs=[view()], dsts=[view() for _ in ds]))
    g.remote_dma_fused(trs, local_sem=T.sem.sent)
    return sum(_bits(mask) for mask, _ in groups)


def _helper(g, core, T, topo, plan):
    j, mask, targets = plan["jobs"][core]
    sent = 0
    for part, need in (("s", plan["plane"]), ("c", plan["count"])):
        g.wait_ge(T.sem["%s%d" % (part, j)], need[(core, j)])
        sent += _send(g, T, topo, j, part, [(mask, targets)])
    g.wait_ge(T.sem.sent, sent)


def rank_program(g, core, T, topo):
    plan = _plan(topo, list(T.cores))
    r = T.rank_of(core)
    if r is None:
        if core in plan["jobs"]:
            _helper(g, core, T, topo, plan)
        return
    sem = T.sem
    ve, te, se, sy = g.vector, g.tensor, g.scalar, g.sync

    def bank(k):
        return T.ps[:, 512 * k:512 * k + HC]

    def quant(q, s, b, k, done):
        ve.quantize_mx(q[:, 128 * k:128 * k + 128], s[:, 128 * k:128 * k + 128],
                       b[:, 512 * k:512 * k + 512]).then_inc(done, 1)

    sy.dma_start(T.xb[:], T.x[:]).then_inc(sem.lx, 16)
    se.dma_start(T.ub[:], T.u[:]).then_inc(sem.lu, 16)
    sy.dma_start(T.vb[:], T.v[:]).then_inc(sem.lv, 16)
    sy.dma_start(T.wb[:], T.w2[:]).then_inc(sem.lw, 16)

    ve.wait_ge(sem.lx, 16)
    quant(T.xq, T.xs, T.xb, 0, sem.qx0)
    ve.wait_ge(sem.lu, 16)
    quant(T.uq, T.us, T.ub, 0, sem.qu0)
    quant(T.uq, T.us, T.ub, 1, sem.qu1)
    quant(T.xq, T.xs, T.xb, 1, sem.qx1)
    ve.wait_ge(sem.lv, 16)
    quant(T.vq, T.vs, T.vb, 0, sem.qv0)
    quant(T.vq, T.vs, T.vb, 1, sem.qv1)

    for k, (name, q, s) in enumerate((("u", T.uq, T.us), ("v", T.vq, T.vs))):
        for h in range(2):
            te.wait_ge(sem["qx%d" % h], 1)
            for i in range(2):
                te.wait_ge(sem["q%s%d" % (name, i)], 1)
                te.matmul_mx(bank(4 * k + 2 * h + i), q[:, 128 * i:128 * i + 128], s[:, 128 * i:128 * i + 128],
                             T.xq[:, HC * h:HC * h + HC], T.xs[:, HC * h:HC * h + HC],
                             True, True).then_inc(sem["m%s%d%d" % (name, i, h)], 1)

    for h in range(2):
        for b in range(4):
            if b % 2 == 0:
                se.wait_ge(sem["mu%d%d" % (b // 2, h)], 1)
            lo = NC * b + HC * h
            se.activation(T.a[:, lo:lo + HC], bank(2 * h + b // 2), ActivationFunctionType.Relu,
                          scale=(C if b % 2 == 0 else -C)).then_inc(sem["r%d%d" % (b, h)], 1)

    for h in range(2):
        for b in range(4):
            ve.wait_ge(sem["r%d%d" % (b, h)], 1)
            if b % 2 == 0:
                ve.wait_ge(sem["mv%d%d" % (b // 2, h)], 1)
            lo = NC * b + HC * h
            ve.tensor_tensor(T.hb[:, 4 * HC * h + b:4 * HC * h + 4 * HC:4], T.a[:, lo:lo + HC],
                             bank(4 + 2 * h + b // 2), AluOpType.mult).then_inc(sem["hm%d" % h], 1)
        ve.wait_ge(sem["hm%d" % h], 4)
        lo = NC * r + HC * h
        ve.quantize_mx(T.hq[:, lo:lo + HC], T.hs[:, lo:lo + HC],
                       T.hb[:, 4 * HC * h:4 * HC * h + 4 * HC]).then_inc(sem["qh%d" % h], 1)

    first = plan["waves"][r][0]
    g.wait_ge(sem.qh0, 1)
    sent = _send(g, T, topo, r, "s", first, 0, HC)
    g.wait_ge(sem.qh1, 1)
    sent += _send(g, T, topo, r, "s", first, HC, NC)
    sent += _send(g, T, topo, r, "c", first)
    for wave in plan["waves"][r][1:]:
        for part in ("s", "c"):
            sent += _send(g, T, topo, r, part, wave)
    g.wait_ge(sem.sent, sent)

    ve.wait_ge(sem.lw, 16)
    for k in range(2):
        w = N * 128 // 2
        ve.quantize_mx(T.wq[:, w * k:w * k + w], T.ws[:, w * k:w * k + w],
                       T.wb[:, 4 * w * k:4 * w * k + 4 * w]).then_inc(sem.qw, 1)

    te.wait_ge(sem.qw, 2)
    te.wait_ge(sem.qh0, 1)
    te.wait_ge(sem.qh1, 1)
    for b in range(4):
        te.wait_ge(sem["r%d0" % b], 1)
    for n, j in enumerate(plan["order"][r]):
        if j != r:
            te.wait_ge(sem["s%d" % j], plan["plane"][(core, j)])
            te.wait_ge(sem["c%d" % j], plan["count"][(core, j)])
        for h in range(2):
            lo = NC * j + HC * h
            mm = te.matmul_mx(bank(h), T.wq[:, 128 * j:128 * j + 128], T.ws[:, 128 * j:128 * j + 128],
                              T.hq[:, lo:lo + HC], T.hs[:, lo:lo + HC], n == 0, n == N - 1)
            if n == N - 1:
                mm.then_inc(sem["y%d" % h], 1)

    ve.wait_ge(sem.y0, 1)
    ve.tensor_copy(T.yb[:, 0:HC], bank(0)).then_inc(sem.yc, 1)
    se.wait_ge(sem.y1, 1)
    se.activation(T.yb[:, HC:NC], bank(1), ActivationFunctionType.Copy).then_inc(sem.yc, 1)
    sy.wait_ge(sem.yc, 2)
    sy.dma_start(T.y[:], T.yb[:]).then_inc(sem.st, 16)
    sy.wait_ge(sem.st, 16)
